import numpy as np
import ml_dtypes


def mxq(x, axis, fmt="e4m3"):
    dtype, down = {"e4m3": (ml_dtypes.float8_e4m3fn, 7), "e5m2": (ml_dtypes.float8_e5m2, 14)}[fmt]
    v = np.moveaxis(np.asarray(x, np.float32).astype(ml_dtypes.bfloat16).astype(np.float64), axis, -1)
    blocks = v.reshape(v.shape[:-1] + (-1, 32))
    amax = np.abs(blocks).max(-1, keepdims=True)
    byte = np.maximum(np.where(amax > 0, np.frexp(amax)[1] - 1 + 127, 0) - down, 1)
    scale = np.exp2(byte - 127.0)
    codes = (blocks / scale).astype(np.float32).astype(dtype).astype(np.float64)
    return np.moveaxis((codes * scale).reshape(v.shape), -1, axis)


WIDE = False


def mx_kscale(k):
    if not WIDE:
        return np.ones(k)
    levels = np.array([30, -30])
    if k % 512:
        return np.exp2(np.random.permutation(np.resize(levels, k // 32))).repeat(32)
    a = np.empty((k // 512, 16))
    for p in range(k // 512):
        a[p, :8] = np.random.permutation(np.resize(levels, 8))
        for g in range(8):
            far = levels[np.abs(levels - a[p, g]) >= 10]
            a[p, g + 8] = far[np.random.randint(len(far))]
    return np.exp2(a.ravel()).repeat(32)


def f64(x):
    return np.asarray(x).astype(np.float64)


def striped(idx):
    return np.tile(np.asarray(idx).reshape(-1, 16).T, (8, 1)).astype(np.uint16)


def unstriped(offs):
    return offs[:16].T.reshape(-1).astype(np.int64)


E2M1 = np.array([0.0, 0.5, 1.0, 1.5, 2.0, 3.0, 4.0, 6.0, -0.0, -0.5, -1.0, -1.5, -2.0, -3.0, -4.0, -6.0])


def pack_weight(w, fmt):
    k, n = w.shape
    w = f64(np.asarray(w, np.float32).astype(ml_dtypes.bfloat16)).reshape(k // 32, 32, n)
    amax = np.abs(w).max(1)
    if fmt in ("e4m3", "e5m2"):
        byte = np.frexp(amax)[1] - 1 + 127 - (7 if fmt == "e4m3" else 14)
    else:
        mant, ex = np.frexp(amax / 6.0)
        byte = np.where(mant > 0.5, ex, ex - 1) + 127
    byte = np.clip(np.where(amax > 0, byte, 1), 1, 254)
    scaled = (w * np.exp2(127.0 - byte)[:, None, :]).reshape(k, n).astype(np.float32)
    by_word = np.ascontiguousarray(scaled.reshape(k // 512, 128, 4, n).transpose(0, 1, 3, 2))
    if fmt in ("e4m3", "e5m2"):
        words = by_word.astype(ml_dtypes.float8_e4m3fn if fmt == "e4m3" else ml_dtypes.float8_e5m2).view(np.uint8)
    else:
        c = by_word.astype(ml_dtypes.float4_e2m1fn).view(np.uint8) & 0xF
        words = (c[..., 0::2] | (c[..., 1::2] << 4)).reshape(k // 512, 128, 2 * n)
    return np.ascontiguousarray(words), np.ascontiguousarray(byte.astype(np.uint8).reshape(k // 512, 16, n))


def unpack_weight(words, scales, fmt):
    g, _, n = scales.shape
    words = np.ascontiguousarray(words).reshape(g, 128, n, -1)
    if fmt in ("e4m3", "e5m2"):
        vals = words.view(ml_dtypes.float8_e4m3fn if fmt == "e4m3" else ml_dtypes.float8_e5m2).astype(np.float64)
    else:
        nib = np.empty((g, 128, n, 4), np.uint8)
        nib[..., 0::2] = words & 0xF
        nib[..., 1::2] = words >> 4
        vals = E2M1[nib]
    vals = vals * np.repeat(np.exp2(scales.astype(np.float64) - 127.0), 8, axis=1)[..., None]
    return vals.transpose(0, 1, 3, 2).reshape(g * 512, n)


def sigmoid(v):
    return 1.0 / (1.0 + np.exp(-v))


def sgn(shape):
    return np.random.uniform(0.5, 2.0, shape) * np.where(np.random.standard_normal(shape) < 0, -1.0, 1.0)


K, T, J, R, F, Z, O, N = 512, 1024, 256, 512, 512, 1024, 128, 256


def setup_inputs():
    n = np.random.standard_normal
    idx = np.random.permutation(T)[:J]
    idx2 = np.random.permutation(Z)[:J]
    idx3 = np.random.permutation(J)[:O]
    idx4 = np.random.permutation(J)[:O]
    idx5 = np.random.permutation(J)[:O]
    idx6 = np.random.permutation(J)[:O]
    idx7 = np.random.permutation(T)[:O]
    fk = mx_kscale(K)
    ff = mx_kscale(F)
    fr = mx_kscale(R)
    xtp = pack_weight(n((K, T)) / fk[:, None], "e4m3")
    xop = pack_weight(n((F, Z)) / ff[:, None], "e2m1")
    wp = pack_weight(n((K, R)) * 1 / np.sqrt(K) * fk[:, None], "e2m1")
    w0p = pack_weight(n((F, R)) * 1 / np.sqrt(F) * ff[:, None], "e5m2")
    w2p = pack_weight(n((F, R)) * 1 / np.sqrt(F) * ff[:, None], "e5m2")
    wbp = pack_weight(n((R, N)) * 1 / np.sqrt(R) / fr[:, None], "e5m2")
    wsp = pack_weight(n((K, N)) * 1 / np.sqrt(K) * fk[:, None], "e5m2")
    return {
        "xt_words": xtp[0],
        "xt_scales": xtp[1],
        "xo_words": xop[0],
        "xo_scales": xop[1],
        "w_words": wp[0],
        "w_scales": wp[1],
        "w0_words": w0p[0],
        "w0_scales": w0p[1],
        "w2_words": w2p[0],
        "w2_scales": w2p[1],
        "sa": (np.random.uniform(0.5, 1.6, (R, 1)) * fr[:, None]).astype(np.float32),
        "sb": (np.random.uniform(0.5, 1.6, (R, 1)) * fr[:, None]).astype(np.float32),
        "sg": (sgn((R, 1))).astype(np.float32),
        "bg": (np.random.uniform(-2.0, 2.0, (R, 1))).astype(np.float32),
        "sh": (sgn((R, 1))).astype(np.float32),
        "bh": (np.random.uniform(-2.0, 2.0, (R, 1))).astype(np.float32),
        "wb_words": wbp[0],
        "wb_scales": wbp[1],
        "ws_words": wsp[0],
        "ws_scales": wsp[1],
        "offs": striped(idx),
        "offs2": striped(idx2),
        "offs3": striped(idx3),
        "offs4": striped(idx4),
        "offs5": striped(idx5),
        "offs6": striped(idx6),
        "offs7": striped(idx7),
    }


def reference(xt_words, xt_scales, xo_words, xo_scales, w_words, w_scales, w0_words, w0_scales, w2_words, w2_scales, sa, sb, sg, bg, sh, bh, wb_words, wb_scales, ws_words, ws_scales, offs, offs2, offs3, offs4, offs5, offs6, offs7):
    idx = unstriped(offs)
    idx2 = unstriped(offs2)
    idx3 = unstriped(offs3)
    idx4 = unstriped(offs4)
    idx5 = unstriped(offs5)
    idx6 = unstriped(offs6)
    idx7 = unstriped(offs7)
    xtu = unpack_weight(xt_words, xt_scales, "e4m3")
    xou = unpack_weight(xo_words, xo_scales, "e2m1")
    wu = unpack_weight(w_words, w_scales, "e2m1")
    w0u = unpack_weight(w0_words, w0_scales, "e5m2")
    w2u = unpack_weight(w2_words, w2_scales, "e5m2")
    wbu = unpack_weight(wb_words, wb_scales, "e5m2")
    wsu = unpack_weight(ws_words, ws_scales, "e5m2")
    xtidxg = xtu[:, idx]
    xoidx2g = xou[:, idx2]
    a = wu.T @ xtidxg + w0u.T @ xoidx2g
    b = w2u.T @ xoidx2g
    u1 = a[:, idx3] * f64(sa) * sigmoid(b[:, idx4] * f64(sg) + f64(bg))
    u2 = b[:, idx5] * f64(sb) * sigmoid(a[:, idx6] * f64(sh) + f64(bh))
    hid = np.maximum(u1, u2)
    hidq = mxq(hid, 0, "e4m3")
    xtidx7g = xtu[:, idx7]
    y = wbu.T @ hidq + wsu.T @ xtidx7g
    return y

@@ -1,0 +1,263 @@
+from contextlib import ExitStack
+
+import concourse.mybir as mybir
+
+K, T, J, R, F, Z, O, N = 512, 1024, 256, 512, 512, 1024, 128, 256
+FLOPS = 2 * (K * R * J + 2 * F * R * J + R * N * O + K * N * O)
+
+F32 = mybir.dt.float32
+BF16 = mybir.dt.bfloat16
+I32 = mybir.dt.int32
+U32 = mybir.dt.uint32
+U16 = mybir.dt.uint16
+U8 = mybir.dt.uint8
+E4M3 = mybir.dt.float8_e4m3fn_x4
+E5M2 = mybir.dt.float8_e5m2_x4
+E2M1 = mybir.dt.float4_e2m1fn_x4
+ACT = mybir.ActivationFunctionType
+ALU = mybir.AluOpType
+
+P = 128
+PACK = 4
+QUADS = 4
+ROWS = 4
+QUAD = 32
+
+
+def tile_list_gatedcross_noted_further_plain_kernel(
+    tc, xt_words, xt_scales, xo_words, xo_scales, w_words, w_scales, w0_words, w0_scales, w2_words, w2_scales,
+    sa, sb, sg, bg, sh, bh, wb_words, wb_scales, ws_words, ws_scales,
+    offs, offs2, offs3, offs4, offs5, offs6, offs7, out,
+):
+    nc = tc.nc
+    with ExitStack() as ctx:
+        keep = ctx.enter_context(tc.tile_pool(name="keep", bufs=1))
+        psum = ctx.enter_context(tc.psum_pool(name="psum", bufs=1))
+
+        def sbuf(name, shape, dtype, tag=""):
+            return keep.tile(shape, dtype, name=name, tag=tag or name, align_bytes=64)
+
+        def load_list(name, src):
+            tile = keep.tile(list(src.shape), U16, name=name)
+            nc.sync.dma_start(tile[:], src)
+            return tile
+
+        def load_words(queue, name, src, columns, dtype):
+            tile = sbuf(name, [P, columns], dtype)
+            flat = src[0] if src.ndim == 3 else src[0].rearrange("p n t -> p (n t)")
+            queue.dma_start(tile[:].bitcast(I32), flat.bitcast(I32))
+            return tile
+
+        def zeroed_plane(name, columns, engine=nc.vector):
+            tile = sbuf(name, [P, columns], U8)
+            engine.memset(tile[:].bitcast(I32), 0)
+            return tile
+
+        def load_staged(stage, first, src):
+            columns = src.shape[2]
+            nc.sync.dma_start(
+                stage[:, :, first : first + columns].bitcast(I32),
+                src[0].rearrange("(q r) n -> r q n", r=ROWS).bitcast(I32),
+            )
+
+        def load_plane(queue, plane, first, src):
+            columns = src.shape[2]
+            for q in range(QUADS):
+                queue.dma_start(
+                    plane[:, first : first + columns].bitcast(I32)[QUAD * q : QUAD * q + ROWS, :],
+                    src[0, ROWS * q : ROWS * q + ROWS, :].bitcast(I32),
+                )
+
+        def spread(plane, stage):
+            for q in range(QUADS):
+                nc.vector.tensor_copy(
+                    plane[:].bitcast(I32)[QUAD * q : QUAD * q + ROWS, :], stage[:, q, :].bitcast(I32)
+                )
+
+        def load_rows(name, src, queue=nc.sync):
+            tile = keep.tile([P, PACK], F32, name=name)
+            queue.dma_start(tile[:], src.rearrange("(p t) o -> p (t o)", t=PACK))
+            return tile
+
+        warm_in = keep.tile([P, 1], F32, name="warm_in")
+        warm_out = keep.tile([P, 1], F32, name="warm_out")
+        nc.gpsimd.memset(warm_in[:], 0.0)
+        nc.scalar.activation(warm_out[:], warm_in[:], ACT.Sigmoid)
+
+        xo_plane = zeroed_plane("xo_plane", Z)
+        w2_plane = zeroed_plane("w2_plane", R)
+        w0w_plane = zeroed_plane("w0w_plane", 2 * R)
+        xt_plane = zeroed_plane("xt_plane", T, nc.gpsimd)
+        out_plane = zeroed_plane("out_plane", 2 * N)
+
+        w2_stage = keep.tile([ROWS, QUADS, R], U8, name="w2_stage")
+        load_staged(w2_stage, 0, w2_scales)
+        xo_stage = keep.tile([ROWS, QUADS, Z], U8, name="xo_stage")
+        load_staged(xo_stage, 0, xo_scales)
+        l2 = load_list("l2", offs2)
+        xo_w = load_words(nc.sync, "xo_w", xo_words, Z, U16)
+        w2_w = load_words(nc.sync, "w2_w", w2_words, R, U32)
+        w0_w = load_words(nc.sync, "w0_w", w0_words, R, U32)
+        w_w = load_words(nc.sync, "w_w", w_words, R, U16)
+        xt_w = load_words(nc.sync, "xt_w", xt_words, T, U32)
+        load_plane(nc.gpsimd, xt_plane, 0, xt_scales)
+
+        w0w_stage = keep.tile([ROWS, QUADS, 2 * R], U8, name="w0w_stage")
+        load_staged(w0w_stage, 0, w0_scales)
+        load_staged(w0w_stage, R, w_scales)
+        l4 = load_list("l4", offs4)
+        sg_t = load_rows("sg_t", sg)
+        bg_t = load_rows("bg_t", bg)
+        l1 = load_list("l1", offs)
+        l7 = load_list("l7", offs7)
+        l5 = load_list("l5", offs5)
+        sb_t = load_rows("sb_t", sb)
+        l3 = load_list("l3", offs3)
+        sa_t = load_rows("sa_t", sa)
+        l6 = load_list("l6", offs6)
+        sh_t = load_rows("sh_t", sh)
+        bh_t = load_rows("bh_t", bh)
+        ws_w = load_words(nc.sync, "ws_w", ws_words, N, U32)
+        wb_w = load_words(nc.sync, "wb_w", wb_words, N, U32)
+        load_plane(nc.sync, out_plane, 0, ws_scales)
+        load_plane(nc.sync, out_plane, N, wb_scales)
+
+        def deal_words(name, words):
+            dealt = sbuf(name, [P, R], U32)
+            nc.scalar.copy(
+                dealt[:].rearrange("p (t m) -> p m t", t=PACK), words[:].rearrange("p (m t) -> p m t", t=PACK)
+            )
+            return dealt
+
+        def deal_scales(name, plane, count):
+            dealt = sbuf(name, [P, count * R], U8)
+            nc.vector.tensor_copy(
+                dealt[:].rearrange("p (w t m) -> p w t m", w=count, t=PACK),
+                plane[:].rearrange("p (w m t) -> p w t m", w=count, t=PACK),
+            )
+            return dealt
+
+        def gather(name, table, offsets, count, dtype):
+            picked = sbuf(name, [P, count], dtype)
+            nc.vector.tensor_copy(picked[:], table[:].indirect(offsets[:]))
+            return picked
+
+        w2_d = deal_words("w2_d", w2_w)
+        spread(w2_plane, w2_stage)
+        spread(xo_plane, xo_stage)
+        w2_sd = deal_scales("w2_sd", w2_plane, 1)
+        xo_g = gather("xo_g", xo_w, l2, J, U16)
+        xo_sg = gather("xo_sg", xo_plane, l2, J, U8)
+
+        b_ps = [psum.tile([P, J], F32, name=f"b_ps{t}", tag=f"bank{t}") for t in range(PACK)]
+        for t in range(PACK):
+            cols = slice(P * t, P * (t + 1))
+            nc.tensor.matmul_mx(
+                out=b_ps[t][:], lhsT=w2_d[:, cols].bitcast(E5M2), lhsT_scale=w2_sd[:, cols],
+                rhs=xo_g[:].bitcast(E2M1), rhs_scale=xo_sg[:], start=True, stop=True,
+            )
+
+        w0_d = deal_words("w0_d", w0_w)
+        w_d = sbuf("w_d", [P, R], U16)
+        nc.scalar.copy(
+            w_d[:].rearrange("p (t m) -> p t m", t=PACK), w_w[:].rearrange("p (m t) -> p t m", t=PACK)
+        )
+
+        last = PACK - 1
+        spread(w0w_plane, w0w_stage)
+        w0w_sd = deal_scales("w0w_sd", w0w_plane, 2)
+
+        b_sb = [sbuf(f"b_sb{t}", [P, J], F32, tag="w0w_plane" if t == last else "") for t in range(PACK)]
+        a_sb = [sbuf(f"a_sb{t}", [P, J], F32) for t in range(PACK)]
+        a_scaled = keep.tile([P, PACK, O], F32, name="a_scaled")
+        b_gate = keep.tile([P, PACK, O], F32, name="b_gate")
+        b_scaled = keep.tile([P, PACK, O], F32, name="b_scaled")
+        a_gate = keep.tile([P, PACK, O], F32, name="a_gate")
+        u1 = keep.tile([P, PACK, O], F32, name="u1")
+        u2 = keep.tile([P, PACK, O], F32, name="u2")
+
+        for t in range(last):
+            nc.scalar.copy(b_sb[t][:], b_ps[t][:])
+        nc.vector.tensor_copy(b_sb[last][:], b_ps[last][:])
+        for t in range(PACK):
+            nc.scalar.activation(
+                b_gate[:, t, :], b_sb[t][:].indirect(l4[:]), ACT.Sigmoid,
+                bias=bg_t[:, t : t + 1], scale=sg_t[:, t : t + 1],
+            )
+        for t in range(PACK):
+            nc.scalar.activation(b_scaled[:, t, :], b_sb[t][:].indirect(l5[:]), ACT.Copy, scale=sb_t[:, t : t + 1])
+
+        xt_g = gather("xt_g", xt_w, l1, J, U32)
+        xt_sg = gather("xt_sg", xt_plane, l1, J, U8)
+        xt7_sg = gather("xt7_sg", xt_plane, l7, O, U8)
+        xt7_g = gather("xt7_g", xt_w, l7, O, U32)
+
+        a_ps = [psum.tile([P, J], F32, name=f"a_ps{t}", tag=f"bank{PACK + t}") for t in range(PACK)]
+        for t in range(PACK):
+            cols = slice(P * t, P * (t + 1))
+            nc.tensor.matmul_mx(
+                out=a_ps[t][:], lhsT=w0_d[:, cols].bitcast(E5M2), lhsT_scale=w0w_sd[:, cols],
+                rhs=xo_g[:].bitcast(E2M1), rhs_scale=xo_sg[:], start=True, stop=False,
+            )
+        for t in range(PACK):
+            cols = slice(P * t, P * (t + 1))
+            nc.tensor.matmul_mx(
+                out=a_ps[t][:], lhsT=w_d[:, cols].bitcast(E2M1), lhsT_scale=w0w_sd[:, R + P * t : R + P * (t + 1)],
+                rhs=xt_g[:].bitcast(E4M3), rhs_scale=xt_sg[:], start=False, stop=True,
+            )
+        for t in range(PACK):
+            nc.vector.tensor_copy(a_sb[t][:], a_ps[t][:])
+        halves = [slice(0, O // 2), slice(O // 2, O)]
+        for t in range(PACK):
+            nc.scalar.activation(a_scaled[:, t, :], a_sb[t][:].indirect(l3[:]), ACT.Copy, scale=sa_t[:, t : t + 1])
+        for t in range(PACK):
+            for o in halves if t == last else [slice(0, O)]:
+                nc.scalar.activation(
+                    a_gate[:, t, o], a_sb[t][:].indirect(l6[:, o.start // 16 : o.stop // 16]), ACT.Sigmoid,
+                    bias=bh_t[:, t : t + 1], scale=sh_t[:, t : t + 1],
+                )
+
+        y_ps = [psum.tile([P, O], F32, name=f"y_ps{h}", tag=f"bank{h}") for h in range(N // P)]
+        for h in range(N // P):
+            cols = slice(P * h, P * (h + 1))
+            nc.tensor.matmul_mx(
+                out=y_ps[h][:], lhsT=ws_w[:, cols].bitcast(E5M2), lhsT_scale=out_plane[:, cols],
+                rhs=xt7_g[:].bitcast(E4M3), rhs_scale=xt7_sg[:], start=True, stop=False,
+            )
+
+        hid = sbuf("hid", [P, O, PACK], BF16)
+        hid_q = sbuf("hid_q", [P, O], U32)
+        hid_s = sbuf("hid_s", [P, O], U8)
+        pairs = [slice(0, 2), slice(2, 4)]
+
+        def larger(ts, o):
+            nc.vector.tensor_tensor(
+                hid[:, o, ts], u1[:, ts, o].rearrange("p t o -> p o t"), u2[:, ts, o].rearrange("p t o -> p o t"), ALU.max
+            )
+
+        for ts in pairs:
+            nc.vector.tensor_tensor(u1[:, ts, :], a_scaled[:, ts, :], b_gate[:, ts, :], ALU.mult)
+        nc.vector.tensor_tensor(u2[:, pairs[0], :], a_gate[:, pairs[0], :], b_scaled[:, pairs[0], :], ALU.mult)
+        larger(pairs[0], slice(0, O))
+        nc.vector.tensor_tensor(u2[:, 2, :], a_gate[:, 2, :], b_scaled[:, 2, :], ALU.mult)
+        for o in halves:
+            nc.vector.tensor_tensor(u2[:, last, o], a_gate[:, last, o], b_scaled[:, last, o], ALU.mult)
+        for o in halves:
+            larger(pairs[1], o)
+        for o in halves:
+            nc.vector.quantize_mx(
+                out=hid_q[:, o].bitcast(E4M3), scales=hid_s[:, o], in_=hid[:, o, :].rearrange("p o t -> p (o t)")
+            )
+
+        for h in range(N // P):
+            cols = slice(P * h, P * (h + 1))
+            nc.tensor.matmul_mx(
+                out=y_ps[h][:], lhsT=wb_w[:, cols].bitcast(E5M2), lhsT_scale=out_plane[:, N + P * h : N + P * (h + 1)],
+                rhs=hid_q[:].bitcast(E4M3), rhs_scale=hid_s[:], start=False, stop=True,
+            )
+        y0 = keep.tile([P, O], F32, name="y0")
+        y1 = keep.tile([P, O], F32, name="y1")
+        nc.vector.tensor_copy(y0[:], y_ps[0][:])
+        nc.sync.dma_start(out[0:P, :], y0[:])
+        nc.scalar.copy(y1[:], y_ps[1][:])
+        nc.scalar.dma_start(out[P : 2 * P, :], y1[:])

@@ -32,6 +32,7 @@ def tile_list_gatedcross_noted_further_plain_kernel(
     nc = tc.nc
     with ExitStack() as ctx:
         keep = ctx.enter_context(tc.tile_pool(name="keep", bufs=1))
+        reuse = ctx.enter_context(tc.tile_pool(name="reuse", bufs=1))
         psum = ctx.enter_context(tc.psum_pool(name="psum", bufs=1))
 
         def sbuf(name, shape, dtype, tag=""):
@@ -56,7 +57,7 @@ def tile_list_gatedcross_noted_further_plain_kernel(
         def load_staged(stage, first, src):
             columns = src.shape[2]
             nc.sync.dma_start(
-                stage[:, :, first : first + columns].bitcast(I32),
+                stage[0:ROWS, :, first : first + columns].bitcast(I32),
                 src[0].rearrange("(q r) n -> r q n", r=ROWS).bitcast(I32),
             )
 
@@ -68,10 +69,10 @@ def tile_list_gatedcross_noted_further_plain_kernel(
                     src[0, ROWS * q : ROWS * q + ROWS, :].bitcast(I32),
                 )
 
-        def spread(plane, stage):
-            for q in range(QUADS):
+        def spread(plane, stage, first=0):
+            for q in range(first, QUADS):
                 nc.vector.tensor_copy(
-                    plane[:].bitcast(I32)[QUAD * q : QUAD * q + ROWS, :], stage[:, q, :].bitcast(I32)
+                    plane.bitcast(I32)[QUAD * q : QUAD * q + ROWS, :], stage[0:ROWS, q, :].bitcast(I32)
                 )
 
         def load_rows(name, src, queue=nc.sync):
@@ -84,30 +85,36 @@ def tile_list_gatedcross_noted_further_plain_kernel(
         nc.gpsimd.memset(warm_in[:], 0.0)
         nc.scalar.activation(warm_out[:], warm_in[:], ACT.Sigmoid)
 
-        xo_plane = zeroed_plane("xo_plane", Z)
+        xo_stage = sbuf("xo_stage", [2 * QUAD, 2, Z], U8)
+        nc.vector.memset(xo_stage[:, 0, :].bitcast(I32), 0)
+        nc.gpsimd.memset(xo_stage[:, 1, :].bitcast(I32), 0)
+        xo_plane = sbuf("xo_plane", [P, Z], U8)
         w2_plane = zeroed_plane("w2_plane", R)
-        w0w_plane = zeroed_plane("w0w_plane", 2 * R)
-        xt_plane = zeroed_plane("xt_plane", T, nc.gpsimd)
+        w0w_stage = reuse.tile([P, QUADS, 2 * R], U8, name="w0w_stage", offset=0)
+        w0w_plane = w0w_stage[:, 0, :]
+        nc.vector.memset(w0w_plane.bitcast(I32), 0)
+        xt_plane = zeroed_plane("xt_plane", T)
         out_plane = zeroed_plane("out_plane", 2 * N)
 
         w2_stage = keep.tile([ROWS, QUADS, R], U8, name="w2_stage")
         load_staged(w2_stage, 0, w2_scales)
-        xo_stage = keep.tile([ROWS, QUADS, Z], U8, name="xo_stage")
-        load_staged(xo_stage, 0, xo_scales)
         l2 = load_list("l2", offs2)
         xo_w = load_words(nc.sync, "xo_w", xo_words, Z, U16)
+        xo_rows = xo_scales[0].rearrange("(u q r) n -> q r u n", u=2, r=ROWS).bitcast(I32)
+        for q in range(2):
+            nc.sync.dma_start(xo_stage[QUAD * q : QUAD * q + ROWS, :, :].bitcast(I32), xo_rows[q])
         w2_w = load_words(nc.sync, "w2_w", w2_words, R, U32)
         w0_w = load_words(nc.sync, "w0_w", w0_words, R, U32)
         w_w = load_words(nc.sync, "w_w", w_words, R, U16)
-        xt_w = load_words(nc.sync, "xt_w", xt_words, T, U32)
-        load_plane(nc.gpsimd, xt_plane, 0, xt_scales)
-
-        w0w_stage = keep.tile([ROWS, QUADS, 2 * R], U8, name="w0w_stage")
+        sg_t = load_rows("sg_t", sg, nc.gpsimd)
+        bg_t = load_rows("bg_t", bg, nc.gpsimd)
+        sh_t = load_rows("sh_t", sh, nc.gpsimd)
+        bh_t = load_rows("bh_t", bh, nc.gpsimd)
         load_staged(w0w_stage, 0, w0_scales)
         load_staged(w0w_stage, R, w_scales)
+        xt_w = load_words(nc.sync, "xt_w", xt_words, T, U32)
         l4 = load_list("l4", offs4)
-        sg_t = load_rows("sg_t", sg)
-        bg_t = load_rows("bg_t", bg)
+        load_plane(nc.sync, xt_plane, 0, xt_scales)
         l1 = load_list("l1", offs)
         l7 = load_list("l7", offs7)
         l5 = load_list("l5", offs5)
@@ -115,8 +122,6 @@ def tile_list_gatedcross_noted_further_plain_kernel(
         l3 = load_list("l3", offs3)
         sa_t = load_rows("sa_t", sa)
         l6 = load_list("l6", offs6)
-        sh_t = load_rows("sh_t", sh)
-        bh_t = load_rows("bh_t", bh)
         ws_w = load_words(nc.sync, "ws_w", ws_words, N, U32)
         wb_w = load_words(nc.sync, "wb_w", wb_words, N, U32)
         load_plane(nc.sync, out_plane, 0, ws_scales)
@@ -133,7 +138,7 @@ def tile_list_gatedcross_noted_further_plain_kernel(
             dealt = sbuf(name, [P, count * R], U8)
             nc.vector.tensor_copy(
                 dealt[:].rearrange("p (w t m) -> p w t m", w=count, t=PACK),
-                plane[:].rearrange("p (w m t) -> p w t m", w=count, t=PACK),
+                plane.rearrange("p (w m t) -> p w t m", w=count, t=PACK),
             )
             return dealt
 
@@ -143,9 +148,12 @@ def tile_list_gatedcross_noted_further_plain_kernel(
             return picked
 
         w2_d = deal_words("w2_d", w2_w)
-        spread(w2_plane, w2_stage)
-        spread(xo_plane, xo_stage)
-        w2_sd = deal_scales("w2_sd", w2_plane, 1)
+        spread(w2_plane[:], w2_stage)
+        w2_sd = deal_scales("w2_sd", w2_plane[:], 1)
+        for half in range(2):
+            nc.vector.tensor_copy(
+                xo_plane[:].bitcast(I32)[2 * QUAD * half : 2 * QUAD * (half + 1), :], xo_stage[:, half, :].bitcast(I32)
+            )
         xo_g = gather("xo_g", xo_w, l2, J, U16)
         xo_sg = gather("xo_sg", xo_plane, l2, J, U8)
 
@@ -164,21 +172,22 @@ def tile_list_gatedcross_noted_further_plain_kernel(
         )
 
         last = PACK - 1
-        spread(w0w_plane, w0w_stage)
+        spread(w0w_plane, w0w_stage, 1)
         w0w_sd = deal_scales("w0w_sd", w0w_plane, 2)
 
-        b_sb = [sbuf(f"b_sb{t}", [P, J], F32, tag="w0w_plane" if t == last else "") for t in range(PACK)]
+        b_sb = [sbuf("b_sb0", [P, J], F32)]
+        b_sb += [reuse.tile([P, J], F32, name=f"b_sb{t}", offset=4 * J * (t - 1)) for t in range(1, PACK)]
         a_sb = [sbuf(f"a_sb{t}", [P, J], F32) for t in range(PACK)]
-        a_scaled = keep.tile([P, PACK, O], F32, name="a_scaled")
-        b_gate = keep.tile([P, PACK, O], F32, name="b_gate")
-        b_scaled = keep.tile([P, PACK, O], F32, name="b_scaled")
-        a_gate = keep.tile([P, PACK, O], F32, name="a_gate")
-        u1 = keep.tile([P, PACK, O], F32, name="u1")
-        u2 = keep.tile([P, PACK, O], F32, name="u2")
+        from_a = keep.tile([P, PACK, 2, O], F32, name="from_a")
+        from_b = keep.tile([P, PACK, 2, O], F32, name="from_b")
+        u = keep.tile([P, PACK, 2, O], F32, name="u")
+        a_scaled, a_gate = from_a[:, :, 0, :], from_a[:, :, 1, :]
+        b_gate, b_scaled = from_b[:, :, 0, :], from_b[:, :, 1, :]
+        u1, u2 = u[:, :, 0, :], u[:, :, 1, :]
 
-        for t in range(last):
-            nc.scalar.copy(b_sb[t][:], b_ps[t][:])
-        nc.vector.tensor_copy(b_sb[last][:], b_ps[last][:])
+        nc.scalar.copy(b_sb[0][:], b_ps[0][:])
+        for t in range(1, PACK):
+            nc.vector.tensor_copy(b_sb[t][:], b_ps[t][:])
         for t in range(PACK):
             nc.scalar.activation(
                 b_gate[:, t, :], b_sb[t][:].indirect(l4[:]), ACT.Sigmoid,
@@ -187,8 +196,8 @@ def tile_list_gatedcross_noted_further_plain_kernel(
         for t in range(PACK):
             nc.scalar.activation(b_scaled[:, t, :], b_sb[t][:].indirect(l5[:]), ACT.Copy, scale=sb_t[:, t : t + 1])
 
-        xt_g = gather("xt_g", xt_w, l1, J, U32)
         xt_sg = gather("xt_sg", xt_plane, l1, J, U8)
+        xt_g = gather("xt_g", xt_w, l1, J, U32)
         xt7_sg = gather("xt7_sg", xt_plane, l7, O, U8)
         xt7_g = gather("xt7_g", xt_w, l7, O, U32)
 
@@ -210,7 +219,6 @@ def tile_list_gatedcross_noted_further_plain_kernel(
         halves = [slice(0, O // 2), slice(O // 2, O)]
         for t in range(PACK):
             nc.scalar.activation(a_scaled[:, t, :], a_sb[t][:].indirect(l3[:]), ACT.Copy, scale=sa_t[:, t : t + 1])
-        for t in range(PACK):
             for o in halves if t == last else [slice(0, O)]:
                 nc.scalar.activation(
                     a_gate[:, t, o], a_sb[t][:].indirect(l6[:, o.start // 16 : o.stop // 16]), ACT.Sigmoid,
@@ -235,11 +243,12 @@ def tile_list_gatedcross_noted_further_plain_kernel(
                 hid[:, o, ts], u1[:, ts, o].rearrange("p t o -> p o t"), u2[:, ts, o].rearrange("p t o -> p o t"), ALU.max
             )
 
-        for ts in pairs:
-            nc.vector.tensor_tensor(u1[:, ts, :], a_scaled[:, ts, :], b_gate[:, ts, :], ALU.mult)
-        nc.vector.tensor_tensor(u2[:, pairs[0], :], a_gate[:, pairs[0], :], b_scaled[:, pairs[0], :], ALU.mult)
+        nc.vector.tensor_tensor(u1[:, pairs[0], :], a_scaled[:, pairs[0], :], b_gate[:, pairs[0], :], ALU.mult)
+        for t in range(2):
+            nc.vector.tensor_tensor(u2[:, t, :], a_gate[:, t, :], b_scaled[:, t, :], ALU.mult)
         larger(pairs[0], slice(0, O))
-        nc.vector.tensor_tensor(u2[:, 2, :], a_gate[:, 2, :], b_scaled[:, 2, :], ALU.mult)
+        nc.vector.tensor_tensor(u[:, 2, :, :], from_a[:, 2, :, :], from_b[:, 2, :, :], ALU.mult)
+        nc.vector.tensor_tensor(u1[:, last, :], a_scaled[:, last, :], b_gate[:, last, :], ALU.mult)
         for o in halves:
             nc.vector.tensor_tensor(u2[:, last, o], a_gate[:, last, o], b_scaled[:, last, o], ALU.mult)
         for o in halves:

@@ -80,19 +80,19 @@ def tile_list_gatedcross_noted_further_plain_kernel(
             queue.dma_start(tile[:], src.rearrange("(p t) o -> p (t o)", t=PACK))
             return tile
 
-        warm_in = keep.tile([P, 1], F32, name="warm_in")
-        warm_out = keep.tile([P, 1], F32, name="warm_out")
-        nc.gpsimd.memset(warm_in[:], 0.0)
-        nc.scalar.activation(warm_out[:], warm_in[:], ACT.Sigmoid)
-
-        xo_stage = sbuf("xo_stage", [2 * QUAD, 2, Z], U8)
-        nc.vector.memset(xo_stage[:, 0, :].bitcast(I32), 0)
-        nc.gpsimd.memset(xo_stage[:, 1, :].bitcast(I32), 0)
+        xo_stage = sbuf("xo_stage", [P, 2, Z], U8)
+        upper = slice(2 * QUAD, P)
+        nc.vector.memset(xo_stage[upper, :, :].bitcast(I32), 0)
         xo_plane = sbuf("xo_plane", [P, Z], U8)
-        w2_plane = zeroed_plane("w2_plane", R)
         w0w_stage = reuse.tile([P, QUADS, 2 * R], U8, name="w0w_stage", offset=0)
         w0w_plane = w0w_stage[:, 0, :]
         nc.vector.memset(w0w_plane.bitcast(I32), 0)
+        w2_plane = zeroed_plane("w2_plane", R)
+        warm_in = keep.tile([P, 1], F32, name="warm_in")
+        warm_out = keep.tile([P, 1], F32, name="warm_out")
+        nc.vector.memset(warm_in[:], 0.0)
+        nc.scalar.activation(warm_out[:], warm_in[:], ACT.Sigmoid)
+
         xt_plane = zeroed_plane("xt_plane", T)
         out_plane = zeroed_plane("out_plane", 2 * N)
 
@@ -102,18 +102,18 @@ def tile_list_gatedcross_noted_further_plain_kernel(
         xo_w = load_words(nc.sync, "xo_w", xo_words, Z, U16)
         xo_rows = xo_scales[0].rearrange("(u q r) n -> q r u n", u=2, r=ROWS).bitcast(I32)
         for q in range(2):
-            nc.sync.dma_start(xo_stage[QUAD * q : QUAD * q + ROWS, :, :].bitcast(I32), xo_rows[q])
+            nc.sync.dma_start(xo_stage[QUAD * (2 + q) : QUAD * (2 + q) + ROWS, :, :].bitcast(I32), xo_rows[q])
         w2_w = load_words(nc.sync, "w2_w", w2_words, R, U32)
-        w0_w = load_words(nc.sync, "w0_w", w0_words, R, U32)
-        w_w = load_words(nc.sync, "w_w", w_words, R, U16)
-        sg_t = load_rows("sg_t", sg, nc.gpsimd)
-        bg_t = load_rows("bg_t", bg, nc.gpsimd)
-        sh_t = load_rows("sh_t", sh, nc.gpsimd)
-        bh_t = load_rows("bh_t", bh, nc.gpsimd)
         load_staged(w0w_stage, 0, w0_scales)
         load_staged(w0w_stage, R, w_scales)
-        xt_w = load_words(nc.sync, "xt_w", xt_words, T, U32)
+        w0_w = load_words(nc.sync, "w0_w", w0_words, R, U32)
+        w_w = load_words(nc.sync, "w_w", w_words, R, U16)
         l4 = load_list("l4", offs4)
+        sg_t = load_rows("sg_t", sg)
+        bg_t = load_rows("bg_t", bg)
+        xt_w = load_words(nc.sync, "xt_w", xt_words, T, U32)
+        sh_t = load_rows("sh_t", sh, nc.gpsimd)
+        bh_t = load_rows("bh_t", bh, nc.gpsimd)
         load_plane(nc.sync, xt_plane, 0, xt_scales)
         l1 = load_list("l1", offs)
         l7 = load_list("l7", offs7)
@@ -152,7 +152,7 @@ def tile_list_gatedcross_noted_further_plain_kernel(
         w2_sd = deal_scales("w2_sd", w2_plane[:], 1)
         for half in range(2):
             nc.vector.tensor_copy(
-                xo_plane[:].bitcast(I32)[2 * QUAD * half : 2 * QUAD * (half + 1), :], xo_stage[:, half, :].bitcast(I32)
+                xo_plane[:].bitcast(I32)[2 * QUAD * half : 2 * QUAD * (half + 1), :], xo_stage[upper, half, :].bitcast(I32)
             )
         xo_g = gather("xo_g", xo_w, l2, J, U16)
         xo_sg = gather("xo_sg", xo_plane, l2, J, U8)
@@ -175,7 +175,7 @@ def tile_list_gatedcross_noted_further_plain_kernel(
         spread(w0w_plane, w0w_stage, 1)
         w0w_sd = deal_scales("w0w_sd", w0w_plane, 2)
 
-        b_sb = [sbuf("b_sb0", [P, J], F32)]
+        b_sb = [sbuf("b_sb0", [P, J], F32, tag="w_w")]
         b_sb += [reuse.tile([P, J], F32, name=f"b_sb{t}", offset=4 * J * (t - 1)) for t in range(1, PACK)]
         a_sb = [sbuf(f"a_sb{t}", [P, J], F32) for t in range(PACK)]
         from_a = keep.tile([P, PACK, 2, O], F32, name="from_a")

from contextlib import ExitStack

import concourse.mybir as mybir

K, T, J, R, F, Z, O, N = 512, 1024, 256, 512, 512, 1024, 128, 256
FLOPS = 2 * (K * R * J + 2 * F * R * J + R * N * O + K * N * O)

F32 = mybir.dt.float32
BF16 = mybir.dt.bfloat16
I32 = mybir.dt.int32
U32 = mybir.dt.uint32
U16 = mybir.dt.uint16
U8 = mybir.dt.uint8
E4M3 = mybir.dt.float8_e4m3fn_x4
E5M2 = mybir.dt.float8_e5m2_x4
E2M1 = mybir.dt.float4_e2m1fn_x4
ACT = mybir.ActivationFunctionType
ALU = mybir.AluOpType

P = 128
PACK = 4
QUADS = 4
ROWS = 4
QUAD = 32


def tile_list_gatedcross_noted_further_plain_kernel(
    tc, xt_words, xt_scales, xo_words, xo_scales, w_words, w_scales, w0_words, w0_scales, w2_words, w2_scales,
    sa, sb, sg, bg, sh, bh, wb_words, wb_scales, ws_words, ws_scales,
    offs, offs2, offs3, offs4, offs5, offs6, offs7, out,
):
    nc = tc.nc
    with ExitStack() as ctx:
        keep = ctx.enter_context(tc.tile_pool(name="keep", bufs=1))
        reuse = ctx.enter_context(tc.tile_pool(name="reuse", bufs=1))
        psum = ctx.enter_context(tc.psum_pool(name="psum", bufs=1))

        def sbuf(name, shape, dtype, tag=""):
            return keep.tile(shape, dtype, name=name, tag=tag or name, align_bytes=64)

        def load_list(name, src):
            tile = keep.tile(list(src.shape), U16, name=name)
            nc.sync.dma_start(tile[:], src)
            return tile

        def load_words(queue, name, src, columns, dtype):
            tile = sbuf(name, [P, columns], dtype)
            flat = src[0] if src.ndim == 3 else src[0].rearrange("p n t -> p (n t)")
            queue.dma_start(tile[:].bitcast(I32), flat.bitcast(I32))
            return tile

        def zeroed_plane(name, columns, engine=nc.vector):
            tile = sbuf(name, [P, columns], U8)
            engine.memset(tile[:].bitcast(I32), 0)
            return tile

        def load_staged(stage, first, src):
            columns = src.shape[2]
            nc.sync.dma_start(
                stage[0:ROWS, :, first : first + columns].bitcast(I32),
                src[0].rearrange("(q r) n -> r q n", r=ROWS).bitcast(I32),
            )

        def load_plane(queue, plane, first, src):
            columns = src.shape[2]
            for q in range(QUADS):
                queue.dma_start(
                    plane[:, first : first + columns].bitcast(I32)[QUAD * q : QUAD * q + ROWS, :],
                    src[0, ROWS * q : ROWS * q + ROWS, :].bitcast(I32),
                )

        def spread(plane, stage, first=0):
            for q in range(first, QUADS):
                nc.vector.tensor_copy(
                    plane.bitcast(I32)[QUAD * q : QUAD * q + ROWS, :], stage[0:ROWS, q, :].bitcast(I32)
                )

        def load_rows(name, src, queue=nc.sync):
            tile = keep.tile([P, PACK], F32, name=name)
            queue.dma_start(tile[:], src.rearrange("(p t) o -> p (t o)", t=PACK))
            return tile

        xo_stage = sbuf("xo_stage", [P, 2, Z], U8)
        upper = slice(2 * QUAD, P)
        nc.vector.memset(xo_stage[upper, :, :].bitcast(I32), 0)
        xo_plane = sbuf("xo_plane", [P, Z], U8)
        w0w_stage = reuse.tile([P, QUADS, 2 * R], U8, name="w0w_stage", offset=0)
        w0w_plane = w0w_stage[:, 0, :]
        nc.vector.memset(w0w_plane.bitcast(I32), 0)
        w2_plane = zeroed_plane("w2_plane", R)
        warm_in = keep.tile([P, 1], F32, name="warm_in")
        warm_out = keep.tile([P, 1], F32, name="warm_out")
        nc.vector.memset(warm_in[:], 0.0)
        nc.scalar.activation(warm_out[:], warm_in[:], ACT.Sigmoid)

        xt_plane = zeroed_plane("xt_plane", T)
        out_plane = zeroed_plane("out_plane", 2 * N)

        w2_stage = keep.tile([ROWS, QUADS, R], U8, name="w2_stage")
        load_staged(w2_stage, 0, w2_scales)
        l2 = load_list("l2", offs2)
        xo_w = load_words(nc.sync, "xo_w", xo_words, Z, U16)
        xo_rows = xo_scales[0].rearrange("(u q r) n -> q r u n", u=2, r=ROWS).bitcast(I32)
        for q in range(2):
            nc.sync.dma_start(xo_stage[QUAD * (2 + q) : QUAD * (2 + q) + ROWS, :, :].bitcast(I32), xo_rows[q])
        w2_w = load_words(nc.sync, "w2_w", w2_words, R, U32)
        load_staged(w0w_stage, 0, w0_scales)
        load_staged(w0w_stage, R, w_scales)
        w0_w = load_words(nc.sync, "w0_w", w0_words, R, U32)
        w_w = load_words(nc.sync, "w_w", w_words, R, U16)
        l4 = load_list("l4", offs4)
        sg_t = load_rows("sg_t", sg)
        bg_t = load_rows("bg_t", bg)
        xt_w = load_words(nc.sync, "xt_w", xt_words, T, U32)
        sh_t = load_rows("sh_t", sh, nc.gpsimd)
        bh_t = load_rows("bh_t", bh, nc.gpsimd)
        load_plane(nc.sync, xt_plane, 0, xt_scales)
        l1 = load_list("l1", offs)
        l7 = load_list("l7", offs7)
        l5 = load_list("l5", offs5)
        sb_t = load_rows("sb_t", sb)
        l3 = load_list("l3", offs3)
        sa_t = load_rows("sa_t", sa)
        l6 = load_list("l6", offs6)
        ws_w = load_words(nc.sync, "ws_w", ws_words, N, U32)
        wb_w = load_words(nc.sync, "wb_w", wb_words, N, U32)
        load_plane(nc.sync, out_plane, 0, ws_scales)
        load_plane(nc.sync, out_plane, N, wb_scales)

        def deal_words(name, words):
            dealt = sbuf(name, [P, R], U32)
            nc.scalar.copy(
                dealt[:].rearrange("p (t m) -> p m t", t=PACK), words[:].rearrange("p (m t) -> p m t", t=PACK)
            )
            return dealt

        def deal_scales(name, plane, count):
            dealt = sbuf(name, [P, count * R], U8)
            nc.vector.tensor_copy(
                dealt[:].rearrange("p (w t m) -> p w t m", w=count, t=PACK),
                plane.rearrange("p (w m t) -> p w t m", w=count, t=PACK),
            )
            return dealt

        def gather(name, table, offsets, count, dtype):
            picked = sbuf(name, [P, count], dtype)
            nc.vector.tensor_copy(picked[:], table[:].indirect(offsets[:]))
            return picked

        w2_d = deal_words("w2_d", w2_w)
        spread(w2_plane[:], w2_stage)
        w2_sd = deal_scales("w2_sd", w2_plane[:], 1)
        for half in range(2):
            nc.vector.tensor_copy(
                xo_plane[:].bitcast(I32)[2 * QUAD * half : 2 * QUAD * (half + 1), :], xo_stage[upper, half, :].bitcast(I32)
            )
        xo_g = gather("xo_g", xo_w, l2, J, U16)
        xo_sg = gather("xo_sg", xo_plane, l2, J, U8)

        b_ps = [psum.tile([P, J], F32, name=f"b_ps{t}", tag=f"bank{t}") for t in range(PACK)]
        for t in range(PACK):
            cols = slice(P * t, P * (t + 1))
            nc.tensor.matmul_mx(
                out=b_ps[t][:], lhsT=w2_d[:, cols].bitcast(E5M2), lhsT_scale=w2_sd[:, cols],
                rhs=xo_g[:].bitcast(E2M1), rhs_scale=xo_sg[:], start=True, stop=True,
            )

        w0_d = deal_words("w0_d", w0_w)
        w_d = sbuf("w_d", [P, R], U16)
        nc.scalar.copy(
            w_d[:].rearrange("p (t m) -> p t m", t=PACK), w_w[:].rearrange("p (m t) -> p t m", t=PACK)
        )

        last = PACK - 1
        spread(w0w_plane, w0w_stage, 1)
        w0w_sd = deal_scales("w0w_sd", w0w_plane, 2)

        b_sb = [sbuf("b_sb0", [P, J], F32, tag="w_w")]
        b_sb += [reuse.tile([P, J], F32, name=f"b_sb{t}", offset=4 * J * (t - 1)) for t in range(1, PACK)]
        a_sb = [sbuf(f"a_sb{t}", [P, J], F32) for t in range(PACK)]
        from_a = keep.tile([P, PACK, 2, O], F32, name="from_a")
        from_b = keep.tile([P, PACK, 2, O], F32, name="from_b")
        u = keep.tile([P, PACK, 2, O], F32, name="u")
        a_scaled, a_gate = from_a[:, :, 0, :], from_a[:, :, 1, :]
        b_gate, b_scaled = from_b[:, :, 0, :], from_b[:, :, 1, :]
        u1, u2 = u[:, :, 0, :], u[:, :, 1, :]

        nc.scalar.copy(b_sb[0][:], b_ps[0][:])
        for t in range(1, PACK):
            nc.vector.tensor_copy(b_sb[t][:], b_ps[t][:])
        for t in range(PACK):
            nc.scalar.activation(
                b_gate[:, t, :], b_sb[t][:].indirect(l4[:]), ACT.Sigmoid,
                bias=bg_t[:, t : t + 1], scale=sg_t[:, t : t + 1],
            )
        for t in range(PACK):
            nc.scalar.activation(b_scaled[:, t, :], b_sb[t][:].indirect(l5[:]), ACT.Copy, scale=sb_t[:, t : t + 1])

        xt_sg = gather("xt_sg", xt_plane, l1, J, U8)
        xt_g = gather("xt_g", xt_w, l1, J, U32)
        xt7_sg = gather("xt7_sg", xt_plane, l7, O, U8)
        xt7_g = gather("xt7_g", xt_w, l7, O, U32)

        a_ps = [psum.tile([P, J], F32, name=f"a_ps{t}", tag=f"bank{PACK + t}") for t in range(PACK)]
        for t in range(PACK):
            cols = slice(P * t, P * (t + 1))
            nc.tensor.matmul_mx(
                out=a_ps[t][:], lhsT=w0_d[:, cols].bitcast(E5M2), lhsT_scale=w0w_sd[:, cols],
                rhs=xo_g[:].bitcast(E2M1), rhs_scale=xo_sg[:], start=True, stop=False,
            )
        for t in range(PACK):
            cols = slice(P * t, P * (t + 1))
            nc.tensor.matmul_mx(
                out=a_ps[t][:], lhsT=w_d[:, cols].bitcast(E2M1), lhsT_scale=w0w_sd[:, R + P * t : R + P * (t + 1)],
                rhs=xt_g[:].bitcast(E4M3), rhs_scale=xt_sg[:], start=False, stop=True,
            )
        for t in range(PACK):
            nc.vector.tensor_copy(a_sb[t][:], a_ps[t][:])
        halves = [slice(0, O // 2), slice(O // 2, O)]
        for t in range(PACK):
            nc.scalar.activation(a_scaled[:, t, :], a_sb[t][:].indirect(l3[:]), ACT.Copy, scale=sa_t[:, t : t + 1])
            for o in halves if t == last else [slice(0, O)]:
                nc.scalar.activation(
                    a_gate[:, t, o], a_sb[t][:].indirect(l6[:, o.start // 16 : o.stop // 16]), ACT.Sigmoid,
                    bias=bh_t[:, t : t + 1], scale=sh_t[:, t : t + 1],
                )

        y_ps = [psum.tile([P, O], F32, name=f"y_ps{h}", tag=f"bank{h}") for h in range(N // P)]
        for h in range(N // P):
            cols = slice(P * h, P * (h + 1))
            nc.tensor.matmul_mx(
                out=y_ps[h][:], lhsT=ws_w[:, cols].bitcast(E5M2), lhsT_scale=out_plane[:, cols],
                rhs=xt7_g[:].bitcast(E4M3), rhs_scale=xt7_sg[:], start=True, stop=False,
            )

        hid = sbuf("hid", [P, O, PACK], BF16)
        hid_q = sbuf("hid_q", [P, O], U32)
        hid_s = sbuf("hid_s", [P, O], U8)
        pairs = [slice(0, 2), slice(2, 4)]

        def larger(ts, o):
            nc.vector.tensor_tensor(
                hid[:, o, ts], u1[:, ts, o].rearrange("p t o -> p o t"), u2[:, ts, o].rearrange("p t o -> p o t"), ALU.max
            )

        nc.vector.tensor_tensor(u1[:, pairs[0], :], a_scaled[:, pairs[0], :], b_gate[:, pairs[0], :], ALU.mult)
        for t in range(2):
            nc.vector.tensor_tensor(u2[:, t, :], a_gate[:, t, :], b_scaled[:, t, :], ALU.mult)
        larger(pairs[0], slice(0, O))
        nc.vector.tensor_tensor(u[:, 2, :, :], from_a[:, 2, :, :], from_b[:, 2, :, :], ALU.mult)
        nc.vector.tensor_tensor(u1[:, last, :], a_scaled[:, last, :], b_gate[:, last, :], ALU.mult)
        for o in halves:
            nc.vector.tensor_tensor(u2[:, last, o], a_gate[:, last, o], b_scaled[:, last, o], ALU.mult)
        for o in halves:
            larger(pairs[1], o)
        for o in halves:
            nc.vector.quantize_mx(
                out=hid_q[:, o].bitcast(E4M3), scales=hid_s[:, o], in_=hid[:, o, :].rearrange("p o t -> p (o t)")
            )

        for h in range(N // P):
            cols = slice(P * h, P * (h + 1))
            nc.tensor.matmul_mx(
                out=y_ps[h][:], lhsT=wb_w[:, cols].bitcast(E5M2), lhsT_scale=out_plane[:, N + P * h : N + P * (h + 1)],
                rhs=hid_q[:].bitcast(E4M3), rhs_scale=hid_s[:], start=False, stop=True,
            )
        y0 = keep.tile([P, O], F32, name="y0")
        y1 = keep.tile([P, O], F32, name="y1")
        nc.vector.tensor_copy(y0[:], y_ps[0][:])
        nc.sync.dma_start(out[0:P, :], y0[:])
        nc.scalar.copy(y1[:], y_ps[1][:])
        nc.scalar.dma_start(out[P : 2 * P, :], y1[:])
